import numpy as np
import ml_dtypes


def mxq(x, axis, fmt="e4m3"):
    dtype, down = {"e4m3": (ml_dtypes.float8_e4m3fn, 7), "e5m2": (ml_dtypes.float8_e5m2, 14)}[fmt]
    v = np.moveaxis(np.asarray(x, np.float32).astype(ml_dtypes.bfloat16).astype(np.float64), axis, -1)
    blocks = v.reshape(v.shape[:-1] + (-1, 32))
    amax = np.abs(blocks).max(-1, keepdims=True)
    byte = np.maximum(np.where(amax > 0, np.frexp(amax)[1] - 1 + 127, 0) - down, 1)
    scale = np.exp2(byte - 127.0)
    codes = (blocks / scale).astype(np.float32).astype(dtype).astype(np.float64)
    return np.moveaxis((codes * scale).reshape(v.shape), -1, axis)


WIDE = False


def mx_kscale(k):
    if not WIDE:
        return np.ones(k)
    levels = np.array([10, -10, 5, -5, 0])
    if k % 512:
        return np.exp2(np.random.permutation(np.resize(levels, k // 32))).repeat(32)
    a = np.empty((k // 512, 16))
    for p in range(k // 512):
        a[p, :8] = np.random.permutation(np.resize(levels, 8))
        for g in range(8):
            far = levels[np.abs(levels - a[p, g]) >= 10]
            a[p, g + 8] = far[np.random.randint(len(far))]
    return np.exp2(a.ravel()).repeat(32)


def f64(x):
    return np.asarray(x).astype(np.float64)


def striped8(idx):
    return np.asarray(idx).reshape(8, -1, 16).transpose(0, 2, 1).reshape(128, -1).astype(np.uint16)


def unstriped8(offs):
    return offs.reshape(8, 16, -1).transpose(0, 2, 1).reshape(8, -1).astype(np.int64)


def pick8(x, idx, run):
    r = np.arange(len(x))
    return x[r[:, None], idx[r % (8 * run) // run]]


E2M1 = np.array([0.0, 0.5, 1.0, 1.5, 2.0, 3.0, 4.0, 6.0, -0.0, -0.5, -1.0, -1.5, -2.0, -3.0, -4.0, -6.0])


def pack_weight(w, fmt):
    k, n = w.shape
    w = f64(np.asarray(w, np.float32).astype(ml_dtypes.bfloat16)).reshape(k // 32, 32, n)
    amax = np.abs(w).max(1)
    if fmt == "e4m3":
        byte = np.frexp(amax)[1] - 1 + 127 - 7
    else:
        mant, ex = np.frexp(amax / 6.0)
        byte = np.where(mant > 0.5, ex, ex - 1) + 127
    byte = np.clip(np.where(amax > 0, byte, 1), 1, 254)
    scaled = (w * np.exp2(127.0 - byte)[:, None, :]).reshape(k, n).astype(np.float32)
    by_word = np.ascontiguousarray(scaled.reshape(k // 512, 128, 4, n).transpose(0, 1, 3, 2))
    if fmt == "e4m3":
        words = by_word.astype(ml_dtypes.float8_e4m3fn).view(np.uint8)
    else:
        c = by_word.astype(ml_dtypes.float4_e2m1fn).view(np.uint8) & 0xF
        words = (c[..., 0::2] | (c[..., 1::2] << 4)).reshape(k // 512, 128, 2 * n)
    return np.ascontiguousarray(words), np.ascontiguousarray(byte.astype(np.uint8).reshape(k // 512, 16, n))


def unpack_weight(words, scales, fmt):
    g, _, n = scales.shape
    words = np.ascontiguousarray(words).reshape(g, 128, n, -1)
    if fmt == "e4m3":
        vals = words.view(ml_dtypes.float8_e4m3fn).astype(np.float64)
    else:
        nib = np.empty((g, 128, n, 4), np.uint8)
        nib[..., 0::2] = words & 0xF
        nib[..., 1::2] = words >> 4
        vals = E2M1[nib]
    vals = vals * np.repeat(np.exp2(scales.astype(np.float64) - 127.0), 8, axis=1)[..., None]
    return vals.transpose(0, 1, 3, 2).reshape(g * 512, n)


D, T, I, Q = 512, 1024, 512, 128


def setup_inputs():
    n = np.random.standard_normal
    idx = np.stack([np.random.permutation(T)[:I] for _ in range(8)])
    idx2 = np.stack([np.random.permutation(T)[:I] for _ in range(8)])
    idx3 = np.stack([np.random.permutation(T)[:I] for _ in range(8)])
    idx4 = np.stack([np.random.permutation(T)[:I] for _ in range(8)])
    fd = mx_kscale(D)
    keysp = pack_weight(n((D, T)) / fd[:, None], "e2m1")
    return {
        "query": (n((D, Q)) * 1.2 / np.sqrt(D) * fd[:, None]).astype(np.float32),
        "keys_words": keysp[0],
        "keys_scales": keysp[1],
        "lam": (np.random.uniform(0.8, 1.8, (Q, 1))).astype(np.float32),
        "old": (1.0 * n((Q, T))).astype(np.float32),
        "offs": striped8(idx),
        "offs2": striped8(idx2),
        "offs3": striped8(idx3),
        "offs4": striped8(idx4),
    }


def reference(query, keys_words, keys_scales, lam, old, offs, offs2, offs3, offs4):
    idx = unstriped8(offs)
    idx2 = unstriped8(offs2)
    idx3 = unstriped8(offs3)
    idx4 = unstriped8(offs4)
    keysu = unpack_weight(keys_words, keys_scales, "e2m1")
    queryq = mxq(f64(query), 0, "e4m3")
    a = queryq.T @ keysu
    lo2 = np.minimum(pick8(a, idx, 16), pick8(a, idx2, 16))
    hi2 = np.maximum(pick8(a, idx, 16), pick8(a, idx2, 16))
    w = np.maximum(lo2, np.minimum(hi2, pick8(a, idx3, 16))) * f64(lam)
    f1 = np.zeros((Q, T))
    f1[np.arange(Q)[:, None], idx[np.arange(Q) % 128 // 16]] = w
    f2 = f1 + f64(old)
    y = pick8(f2, idx4, 16)
    return y

from contextlib import ExitStack

import concourse.mybir as mybir

D, T, SLOTS, Q = 512, 1024, 512, 128
FLOPS = 2 * D * T * Q

F32 = mybir.dt.float32
BF16 = mybir.dt.bfloat16
I32 = mybir.dt.int32
U32 = mybir.dt.uint32
U16 = mybir.dt.uint16
U8 = mybir.dt.uint8
FP8X4 = mybir.dt.float8_e4m3fn_x4
FP4X4 = mybir.dt.float4_e2m1fn_x4
ALU = mybir.AluOpType
COPY = mybir.ActivationFunctionType.Copy

P = 128
PACK = 4
WIDTHS = (256, 256, 256, 128, 128)
ON_SCALAR = (0, 2)
HALF = SLOTS // 2
LIST_COLS = SLOTS // 16


def tile_attend_middle_lean_through_heads_kernel(tc, query, keys_words, keys_scales, lam, old, offs, offs2, offs3, offs4, out):
    nc = tc.nc
    with ExitStack() as ctx:
        sb = ctx.enter_context(tc.tile_pool(name="sb", bufs=1))
        ps = ctx.enter_context(tc.psum_pool(name="ps", bufs=1))

        k_scales = sb.tile([P, T], U8, name="k_scales", align_bytes=64)
        nc.vector.memset(k_scales[:].bitcast(I32), 0)
        f1 = sb.tile([P, T], F32, name="f1")
        nc.vector.memset(f1[:], 0.0)

        q_raw = sb.tile([P, PACK, Q], F32, name="q_raw", tag="staged")
        nc.sync.dma_start(out=q_raw[:], in_=query.rearrange("(p j) q -> p j q", j=PACK))
        scale_rows = keys_scales[0].rearrange("(u r) c -> r u c", r=4)
        for r in range(4):
            nc.sync.dma_start(out=k_scales[r:P:32, :].bitcast(I32), in_=scale_rows[r].bitcast(I32))
        k_words = sb.tile([P, 2 * T], U8, name="k_words", align_bytes=64)
        nc.sync.dma_start(out=k_words[:].bitcast(I32), in_=keys_words[0].bitcast(I32))
        lam_col = sb.tile([P, 1], F32, name="lam_col")
        nc.gpsimd.dma_start(out=lam_col[:], in_=lam)
        lists = []
        for n, src in enumerate((offs, offs2, offs3, offs4)):
            tile = sb.tile([P, LIST_COLS], U16, name="list%d" % n)
            nc.sync.dma_start(tile[:], src)
            lists.append(tile)

        lam_rows = sb.tile([P, HALF], F32, name="lam_rows")
        nc.scalar.activation(lam_rows[:], lam_col[:].to_broadcast([P, HALF]), COPY)

        q_bf = sb.tile([P, Q, PACK], BF16, name="q_bf", align_bytes=64)
        nc.vector.tensor_copy(out=q_bf[:, 0:80, :], in_=q_raw[:, :, 0:80].rearrange("p j q -> p q j"))
        nc.scalar.activation(q_bf[:, 80:Q, :], q_raw[:, :, 80:Q].rearrange("p j q -> p q j"), COPY)
        old_sb = sb.tile([P, T], F32, name="old_sb", tag="staged")
        nc.sync.dma_start(out=old_sb[:], in_=old)
        q_codes = sb.tile([P, Q], U32, name="q_codes", align_bytes=64)
        q_scales = sb.tile([P, Q], U8, name="q_scales", align_bytes=64)
        nc.vector.quantize_mx(out=q_codes[:].bitcast(FP8X4), scales=q_scales[:], in_=q_bf[:].rearrange("p q j -> p (q j)"))

        a = sb.tile([P, T], F32, name="a")
        c0 = 0
        for n, width in enumerate(WIDTHS):
            bank = ps.tile([P, width], F32, name="bank%d" % n)
            nc.tensor.matmul_mx(out=bank[:], lhsT=q_codes[:].bitcast(FP8X4), lhsT_scale=q_scales[:],
                                rhs=k_words[:, 2 * c0 : 2 * (c0 + width)].bitcast(FP4X4), rhs_scale=k_scales[:, c0 : c0 + width],
                                start=True, stop=True)
            if n in ON_SCALAR:
                nc.scalar.activation(a[:, c0 : c0 + width], bank[:], COPY)
            else:
                nc.vector.tensor_copy(out=a[:, c0 : c0 + width], in_=bank[:])
            c0 = c0 + width

        def part(lst, s0, n):
            return lst[:, s0 // 16 : (s0 + n) // 16]

        def look_up(n, h, on_vector=False):
            picked = sb.tile([P, HALF], F32, name="g%d_%d" % (n, h))
            window = a[:].indirect(part(lists[n], h * HALF, HALF))
            if on_vector:
                nc.vector.tensor_copy(out=picked[:], in_=window)
            else:
                nc.scalar.activation(picked[:], window, COPY)
            return picked

        def scatter(mid, s0, n):
            nc.vector.tensor_tensor(f1[:].indirect(part(lists[0], s0, n)), mid[:], lam_rows[:, 0:n], ALU.mult)

        QUART = HALF // 2
        g = [look_up(0, 0), look_up(2, 0, on_vector=True), look_up(1, 0)]
        hi = sb.tile([P, HALF], F32, name="hi0")
        lo = sb.tile([P, HALF], F32, name="lo0")
        hilo = sb.tile([P, 2 * HALF], F32, name="hilo1")
        cap_a = hilo[:, HALF - QUART // 2 : HALF + QUART // 2]
        cap_b = sb.tile([P, QUART], F32, name="cap0b")
        mid_a = sb.tile([P, QUART], F32, name="mid0a")
        mid_b = sb.tile([P, QUART], F32, name="mid0b")
        nc.vector.tensor_tensor(hi[:], g[0][:], g[1][:], ALU.max)
        nc.vector.tensor_tensor(lo[:], g[0][:], g[1][:], ALU.min)
        nc.vector.tensor_tensor(cap_a, hi[:, 0:QUART], g[2][:, 0:QUART], ALU.min)
        nc.vector.tensor_tensor(cap_b[:], hi[:, QUART:HALF], g[2][:, QUART:HALF], ALU.min)
        nc.vector.tensor_tensor(mid_a[:], lo[:, 0:QUART], cap_a, ALU.max)
        nc.vector.tensor_tensor(mid_b[:], lo[:, QUART:HALF], cap_b[:], ALU.max)
        scatter(mid_a, 0, QUART)

        g = [look_up(n, 1) for n in range(3)]
        hi = hilo[:, 0:HALF]
        lo = hilo[:, HALF : 2 * HALF]
        cap = sb.tile([P, HALF], F32, name="cap1")
        mid1 = sb.tile([P, HALF], F32, name="mid1")
        nc.vector.tensor_tensor(hi, g[0][:], g[1][:], ALU.max)
        nc.vector.tensor_tensor(lo, g[0][:], g[1][:], ALU.min)
        nc.vector.tensor_tensor(cap[:], hi, g[2][:], ALU.min)
        scatter(mid_b, QUART, QUART)
        nc.vector.tensor_tensor(mid1[:], lo, cap[:], ALU.max)
        scatter(mid1, HALF, HALF)

        f2 = sb.tile([P, T], F32, name="f2")
        nc.vector.tensor_tensor(f2[:], f1[:], old_sb[:], ALU.add)
        y0 = sb.tile([P, HALF], F32, name="y0")
        y1 = sb.tile([P, HALF], F32, name="y1")
        nc.vector.tensor_copy(out=y0[:], in_=f2[:].indirect(part(lists[3], 0, HALF)))
        nc.sync.dma_start(out=out[:, 0:HALF], in_=y0[:])
        nc.scalar.activation(y1[:], f2[:].indirect(part(lists[3], HALF, HALF)), COPY)
        nc.scalar.dma_start(out=out[:, HALF:SLOTS], in_=y1[:])
